import numpy as np
import ml_dtypes

BF16 = ml_dtypes.bfloat16


def bf(x):
    return np.asarray(x, np.float32).astype(BF16)


def f32(x):
    return np.asarray(x, np.float32)


def f64(x):
    return np.asarray(x).astype(np.float64)


def striped(idx):
    return np.concatenate([l.reshape(-1, 16).T for l in idx])


def rows(idx, k):
    return np.tile(np.repeat(idx, 16, axis=0), (k // (16 * 8), 1))


def look(tab, idx):
    return np.take_along_axis(f64(tab), rows(idx, len(tab)), axis=1)


K, S, D, V, N = 128, 2048, 1, 1536, 1536


def setup_inputs():
    return {"tab": bf(0.7 * np.random.standard_normal((D, K, S))), "base": bf(np.random.standard_normal((K, V))), "offs": striped(np.random.randint(0, S, (8, N)))}


def reference(tab, base, offs):
    idx = np.stack([g.T.reshape(-1) for g in np.split(offs, 8)])
    x = f64(base) + sum(look(tab[d], idx[:, d * V:(d + 1) * V]) for d in range(D))
    return x

@@ -1,0 +1,35 @@
+import concourse.mybir as mybir
+
+F32 = mybir.dt.float32
+BF16 = mybir.dt.bfloat16
+U16 = mybir.dt.uint16
+ADD = mybir.AluOpType.add
+
+PIECE = 512
+PER_COLUMN = 16
+
+
+def tile_lookup_res_add_out_kernel(tc, tab, base, offs, out):
+    nc = tc.nc
+    rows, codewords = tab.shape[1], tab.shape[2]
+    n = base.shape[1]
+
+    with tc.tile_pool(name="held", bufs=1) as held, tc.tile_pool(name="sums", bufs=3) as sums:
+        offsets = held.tile([rows, n // PER_COLUMN], U16, name="offsets")
+        nc.sync.dma_start(offsets[:], offs)
+        table_bf16 = held.tile([rows, codewords], BF16, name="table_bf16")
+        nc.sync.dma_start(table_bf16[:], tab[0, :, :])
+        base_bf16 = held.tile([rows, n], BF16, name="base_bf16")
+        nc.scalar.dma_start(base_bf16[:], base)
+
+        table = held.tile([rows, codewords], F32, name="table")
+        nc.vector.tensor_copy(table[:], table_bf16[:])
+        base_f32 = held.tile([rows, n], F32, name="base_f32")
+        for a in range(0, n, PIECE):
+            nc.scalar.copy(base_f32[:, a : a + PIECE], base_bf16[:, a : a + PIECE])
+
+        for a in range(0, n, PIECE):
+            piece = offsets[:, a // PER_COLUMN : (a + PIECE) // PER_COLUMN]
+            x = sums.tile([rows, PIECE], F32, name="x")
+            nc.vector.tensor_tensor(x[:], table[:].indirect(piece), base_f32[:, a : a + PIECE], ADD)
+            nc.sync.dma_start(out[:, a : a + PIECE], x[:])

@@ -15,17 +15,24 @@ def tile_lookup_res_add_out_kernel(tc, tab, base, offs, out):
     n = base.shape[1]
 
     with tc.tile_pool(name="held", bufs=1) as held, tc.tile_pool(name="sums", bufs=3) as sums:
-        offsets = held.tile([rows, n // PER_COLUMN], U16, name="offsets")
-        nc.sync.dma_start(offsets[:], offs)
         table_bf16 = held.tile([rows, codewords], BF16, name="table_bf16")
-        nc.sync.dma_start(table_bf16[:], tab[0, :, :])
         base_bf16 = held.tile([rows, n], BF16, name="base_bf16")
-        nc.scalar.dma_start(base_bf16[:], base)
-
         table = held.tile([rows, codewords], F32, name="table")
-        nc.vector.tensor_copy(table[:], table_bf16[:])
         base_f32 = held.tile([rows, n], F32, name="base_f32")
-        for a in range(0, n, PIECE):
+        offsets = held.tile([rows, n // PER_COLUMN], U16, name="offsets")
+
+        nc.scalar.dma_start(base_bf16[:, :PIECE], base[:, :PIECE])
+        quarter = codewords // 4
+        for a in range(0, codewords, quarter):
+            nc.sync.dma_start(table_bf16[:, a : a + quarter], tab[0, :, a : a + quarter])
+        nc.sync.dma_start(offsets[:], offs)
+        nc.sync.dma_start(base_bf16[:, PIECE:], base[:, PIECE:])
+
+        nc.scalar.copy(base_f32[:, :PIECE], base_bf16[:, :PIECE])
+        for a in range(0, 3 * quarter, quarter):
+            nc.vector.tensor_copy(table[:, a : a + quarter], table_bf16[:, a : a + quarter])
+        nc.scalar.copy(table[:, 3 * quarter :], table_bf16[:, 3 * quarter :])
+        for a in range(PIECE, n, PIECE):
             nc.scalar.copy(base_f32[:, a : a + PIECE], base_bf16[:, a : a + PIECE])
 
         for a in range(0, n, PIECE):

@@ -28,11 +28,9 @@ def tile_lookup_res_add_out_kernel(tc, tab, base, offs, out):
         nc.sync.dma_start(offsets[:], offs)
         nc.sync.dma_start(base_bf16[:, PIECE:], base[:, PIECE:])
 
-        nc.scalar.copy(base_f32[:, :PIECE], base_bf16[:, :PIECE])
-        for a in range(0, 3 * quarter, quarter):
+        for a in range(0, codewords, quarter):
             nc.vector.tensor_copy(table[:, a : a + quarter], table_bf16[:, a : a + quarter])
-        nc.scalar.copy(table[:, 3 * quarter :], table_bf16[:, 3 * quarter :])
-        for a in range(PIECE, n, PIECE):
+        for a in range(0, n, PIECE):
             nc.scalar.copy(base_f32[:, a : a + PIECE], base_bf16[:, a : a + PIECE])
 
         for a in range(0, n, PIECE):

@@ -22,14 +22,14 @@ def tile_lookup_res_add_out_kernel(tc, tab, base, offs, out):
         offsets = held.tile([rows, n // PER_COLUMN], U16, name="offsets")
 
         nc.scalar.dma_start(base_bf16[:, :PIECE], base[:, :PIECE])
-        quarter = codewords // 4
-        for a in range(0, codewords, quarter):
-            nc.sync.dma_start(table_bf16[:, a : a + quarter], tab[0, :, a : a + quarter])
+        half = codewords // 2
+        for a in range(0, codewords, half):
+            nc.sync.dma_start(table_bf16[:, a : a + half], tab[0, :, a : a + half])
         nc.sync.dma_start(offsets[:], offs)
         nc.sync.dma_start(base_bf16[:, PIECE:], base[:, PIECE:])
 
-        for a in range(0, codewords, quarter):
-            nc.vector.tensor_copy(table[:, a : a + quarter], table_bf16[:, a : a + quarter])
+        for a in range(0, codewords, half):
+            nc.vector.tensor_copy(table[:, a : a + half], table_bf16[:, a : a + half])
         for a in range(0, n, PIECE):
             nc.scalar.copy(base_f32[:, a : a + PIECE], base_bf16[:, a : a + PIECE])
 

import concourse.mybir as mybir

F32 = mybir.dt.float32
BF16 = mybir.dt.bfloat16
U16 = mybir.dt.uint16
ADD = mybir.AluOpType.add

PIECE = 512
PER_COLUMN = 16


def tile_lookup_res_add_out_kernel(tc, tab, base, offs, out):
    nc = tc.nc
    rows, codewords = tab.shape[1], tab.shape[2]
    n = base.shape[1]

    with tc.tile_pool(name="held", bufs=1) as held, tc.tile_pool(name="sums", bufs=3) as sums:
        table_bf16 = held.tile([rows, codewords], BF16, name="table_bf16")
        base_bf16 = held.tile([rows, n], BF16, name="base_bf16")
        table = held.tile([rows, codewords], F32, name="table")
        base_f32 = held.tile([rows, n], F32, name="base_f32")
        offsets = held.tile([rows, n // PER_COLUMN], U16, name="offsets")

        nc.scalar.dma_start(base_bf16[:, :PIECE], base[:, :PIECE])
        half = codewords // 2
        for a in range(0, codewords, half):
            nc.sync.dma_start(table_bf16[:, a : a + half], tab[0, :, a : a + half])
        nc.sync.dma_start(offsets[:], offs)
        nc.sync.dma_start(base_bf16[:, PIECE:], base[:, PIECE:])

        for a in range(0, codewords, half):
            nc.vector.tensor_copy(table[:, a : a + half], table_bf16[:, a : a + half])
        for a in range(0, n, PIECE):
            nc.scalar.copy(base_f32[:, a : a + PIECE], base_bf16[:, a : a + PIECE])

        for a in range(0, n, PIECE):
            piece = offsets[:, a // PER_COLUMN : (a + PIECE) // PER_COLUMN]
            x = sums.tile([rows, PIECE], F32, name="x")
            nc.vector.tensor_tensor(x[:], table[:].indirect(piece), base_f32[:, a : a + PIECE], ADD)
            nc.sync.dma_start(out[:, a : a + PIECE], x[:])
